import numpy as np
import ml_dtypes


def mxq(x, axis, fmt="e4m3"):
    dtype, down = {"e4m3": (ml_dtypes.float8_e4m3fn, 7), "e5m2": (ml_dtypes.float8_e5m2, 14)}[fmt]
    v = np.moveaxis(np.asarray(x, np.float32).astype(ml_dtypes.bfloat16).astype(np.float64), axis, -1)
    blocks = v.reshape(v.shape[:-1] + (-1, 32))
    amax = np.abs(blocks).max(-1, keepdims=True)
    byte = np.maximum(np.where(amax > 0, np.frexp(amax)[1] - 1 + 127, 0) - down, 1)
    scale = np.exp2(byte - 127.0)
    codes = (blocks / scale).astype(np.float32).astype(dtype).astype(np.float64)
    return np.moveaxis((codes * scale).reshape(v.shape), -1, axis)


WIDE = False


def mx_kscale(k):
    if not WIDE:
        return np.ones(k)
    levels = np.array([10, -10, 5, -5, 0])
    if k % 512:
        return np.exp2(np.random.permutation(np.resize(levels, k // 32))).repeat(32)
    a = np.empty((k // 512, 16))
    for p in range(k // 512):
        a[p, :8] = np.random.permutation(np.resize(levels, 8))
        for g in range(8):
            far = levels[np.abs(levels - a[p, g]) >= 10]
            a[p, g + 8] = far[np.random.randint(len(far))]
    return np.exp2(a.ravel()).repeat(32)


def f64(x):
    return np.asarray(x).astype(np.float64)


def striped(idx):
    return np.tile(idx.reshape(-1, 16).T, (8, 1)).astype(np.uint16)


def unstriped(offs):
    return offs[:16].T.reshape(-1).astype(np.int64)


E2M1 = np.array([0.0, 0.5, 1.0, 1.5, 2.0, 3.0, 4.0, 6.0, -0.0, -0.5, -1.0, -1.5, -2.0, -3.0, -4.0, -6.0])


def pack_weight(w, fmt):
    k, n = w.shape
    w = f64(np.asarray(w, np.float32).astype(ml_dtypes.bfloat16)).reshape(k // 32, 32, n)
    amax = np.abs(w).max(1)
    if fmt == "e4m3":
        byte = np.frexp(amax)[1] - 1 + 127 - 7
    else:
        mant, ex = np.frexp(amax / 6.0)
        byte = np.where(mant > 0.5, ex, ex - 1) + 127
    byte = np.clip(np.where(amax > 0, byte, 1), 1, 254)
    scaled = (w * np.exp2(127.0 - byte)[:, None, :]).reshape(k, n).astype(np.float32)
    by_word = np.ascontiguousarray(scaled.reshape(k // 512, 128, 4, n).transpose(0, 1, 3, 2))
    if fmt == "e4m3":
        words = by_word.astype(ml_dtypes.float8_e4m3fn).view(np.uint8)
    else:
        c = by_word.astype(ml_dtypes.float4_e2m1fn).view(np.uint8) & 0xF
        words = (c[..., 0::2] | (c[..., 1::2] << 4)).reshape(k // 512, 128, 2 * n)
    return np.ascontiguousarray(words), np.ascontiguousarray(byte.astype(np.uint8).reshape(k // 512, 16, n))


def unpack_weight(words, scales, fmt):
    g, _, n = scales.shape
    words = np.ascontiguousarray(words).reshape(g, 128, n, -1)
    if fmt == "e4m3":
        vals = words.view(ml_dtypes.float8_e4m3fn).astype(np.float64)
    else:
        nib = np.empty((g, 128, n, 4), np.uint8)
        nib[..., 0::2] = words & 0xF
        nib[..., 1::2] = words >> 4
        vals = E2M1[nib]
    vals = vals * np.repeat(np.exp2(scales.astype(np.float64) - 127.0), 8, axis=1)[..., None]
    return vals.transpose(0, 1, 3, 2).reshape(g * 512, n)


def gelu(v):
    return 0.5 * v * (1.0 + np.tanh(np.sqrt(2.0 / np.pi) * (v + 0.044715 * v**3)))


K, H, N, T, S, P = 1536, 1024, 768, 2048, 1024, 512

def setup_inputs():
    n = np.random.standard_normal
    s = mx_kscale(K)[:, None]
    u = mx_kscale(H)[:, None]
    d = {}
    d["tab_words"], d["tab_scales"] = pack_weight(n((K, T)) * s, "e2m1")
    d["offs"] = striped(np.random.permutation(T)[:S])
    d["pos1"] = striped(np.random.permutation(S)[:P])
    d["pos2"] = striped(np.random.permutation(S)[:P])
    d["w1"] = (n((K, H)) / K**0.5 / s).astype(np.float32)
    d["gain1"] = np.exp(0.3 * n(H)).astype(np.float32)
    d["gain2"] = (np.exp(0.3 * n(H)) * u[:, 0]).astype(np.float32)
    d["w2_words"], d["w2_scales"] = pack_weight(n((H, N)) / H**0.5 / u, "e2m1")
    return d

def reference(tab_words, tab_scales, offs, pos1, pos2, w1, gain1, gain2, w2_words, w2_scales):
    v = unpack_weight(tab_words, tab_scales, "e2m1")[:, unstriped(offs)]
    h = f64(gain1)[:, None] * (mxq(f64(w1), 0, "e4m3").T @ v)
    diff = h[:, unstriped(pos1)] - h[:, unstriped(pos2)]
    z = f64(gain2)[:, None] * np.tanh(diff)
    w2 = unpack_weight(w2_words, w2_scales, "e2m1")
    out = w2.T @ mxq(z, 0, "e4m3")
    return out

@@ -1,0 +1,279 @@
+from contextlib import ExitStack
+
+import concourse.mybir as mybir
+
+K, H, N, T, S, PAIRS = 1536, 1024, 768, 2048, 1024, 512
+FLOPS = 2 * K * H * S + 2 * H * N * PAIRS
+
+F32 = mybir.dt.float32
+BF16 = mybir.dt.bfloat16
+I32 = mybir.dt.int32
+U32 = mybir.dt.uint32
+U16 = mybir.dt.uint16
+U8 = mybir.dt.uint8
+FP8X4 = mybir.dt.float8_e4m3fn_x4
+FP4X4 = mybir.dt.float4_e2m1fn_x4
+ACT = mybir.ActivationFunctionType
+ALU = mybir.AluOpType
+
+P = 128
+PACK = 4
+PASS = P * PACK
+K_PASSES = K // PASS
+R_PASSES = H // PASS
+BANK = 512
+HALVES = S // BANK
+N_TILES = N // P
+STRIPE = 16
+QUADS = 4
+
+
+def tile_list_glyph_kerning_features_kernel(
+    tc, tab_words, tab_scales, offs, pos1, pos2, w1, gain1, gain2, w2_words, w2_scales, out
+):
+    nc = tc.nc
+    with ExitStack() as ctx:
+        keep = ctx.enter_context(tc.tile_pool(name="keep", bufs=1))
+        stage = ctx.enter_context(tc.tile_pool(name="stage", bufs=K_PASSES))
+        ring = ctx.enter_context(tc.tile_pool(name="ring", bufs=2))
+        psum = ctx.enter_context(tc.psum_pool(name="psum", bufs=1))
+
+        offs_t = keep.tile([P, S // STRIPE], U16, name="offs_t")
+        pos1_t = keep.tile([P, PAIRS // STRIPE], U16, name="pos1_t")
+        pos2_t = keep.tile([P, PAIRS // STRIPE], U16, name="pos2_t")
+        tab_sc = keep.tile([P, T], U8, name="tab_sc", align_bytes=64)
+        tab_w = [keep.tile([P, T], U16, name=f"tab_w{a}", align_bytes=64) for a in range(K_PASSES)]
+        v_sc = [keep.tile([P, S], U8, name=f"v_sc{a}", align_bytes=64) for a in range(K_PASSES)]
+        v_w = [
+            [keep.tile([P, BANK], U16, name=f"v_w{a}_{s}", align_bytes=64) for s in range(HALVES)]
+            for a in range(K_PASSES)
+        ]
+        raw = {}
+        grp = [
+            [keep.tile([P, PACK, P, PACK], BF16, name=f"grp{b}_{a}", align_bytes=64) for a in range(K_PASSES)]
+            for b in range(R_PASSES)
+        ]
+        w1_c = [
+            [keep.tile([P, PASS], U32, name=f"w1_c{b}_{a}", align_bytes=64) for a in range(K_PASSES)]
+            for b in range(R_PASSES)
+        ]
+        w1_s = [
+            [keep.tile([P, PASS], U8, name=f"w1_s{b}_{a}", align_bytes=64) for a in range(K_PASSES)]
+            for b in range(R_PASSES)
+        ]
+        h = [[keep.tile([P, S], F32, name=f"h{b}_{t}") for t in range(PACK)] for b in range(R_PASSES)]
+        g1 = keep.tile([P, R_PASSES, PACK], F32, name="g1")
+        g2 = keep.tile([P, R_PASSES, PACK], F32, name="g2")
+        w2_s = keep.tile([P, R_PASSES, N], U8, name="w2_s", align_bytes=64)
+
+        nc.vector.memset(tab_sc[:].bitcast(I32), 0)
+        for a in range(1, K_PASSES):
+            nc.vector.memset(v_sc[a][:].bitcast(I32), 0)
+        nc.vector.memset(w2_s[:].rearrange("p a c -> p (a c)").bitcast(I32), 0)
+
+        def load_w1(b, a):
+            rows = w1[a * PASS : (a + 1) * PASS, b * PASS : (b + 1) * PASS]
+            raw[b, a] = stage.tile([P, PACK, PASS], F32, name=f"raw{b}_{a}", tag="stage", align_bytes=64)
+            nc.sync.dma_start(out=raw[b, a][:], in_=rows.rearrange("(p j) c -> p j c", j=PACK))
+
+        nc.sync.dma_start(offs_t[:], offs)
+        for q in range(QUADS):
+            nc.sync.dma_start(
+                out=tab_sc[32 * q : 32 * q + 4 * K_PASSES, :].bitcast(I32),
+                in_=tab_scales[:, 4 * q : 4 * q + 4, :].bitcast(I32),
+            )
+        for a in range(K_PASSES):
+            nc.sync.dma_start(out=tab_w[a][:].bitcast(I32), in_=tab_words[a].bitcast(I32))
+            load_w1(0, a)
+            if a == 1:
+                nc.sync.dma_start(out=g1[:], in_=gain1.rearrange("(b p t) -> p b t", b=R_PASSES, t=PACK))
+                nc.sync.dma_start(pos2_t[:], pos2)
+                nc.sync.dma_start(pos1_t[:], pos1)
+        nc.gpsimd.dma_start(out=g2[:], in_=gain2.rearrange("(b p t) -> p b t", b=R_PASSES, t=PACK))
+        for q in range(QUADS):
+            nc.gpsimd.dma_start(
+                out=w2_s[32 * q : 32 * q + 4, :, :].bitcast(I32),
+                in_=w2_scales[:, 4 * q : 4 * q + 4, :].rearrange("a r c -> r a c").bitcast(I32),
+            )
+
+        def round_w1(b, a, m0, m1, on_vector):
+            src = raw[b, a][:].rearrange("p j (m t) -> p m j t", t=PACK)[:, m0:m1]
+            dst = grp[b][a][:].rearrange("p t m j -> p m j t")[:, m0:m1]
+            if on_vector:
+                nc.vector.tensor_copy(out=dst, in_=src)
+            else:
+                nc.scalar.activation(out=dst, in_=src, func=ACT.Copy)
+
+        def quantize_w1(b, a):
+            nc.vector.quantize_mx(
+                out=w1_c[b][a][:].bitcast(FP8X4),
+                scales=w1_s[b][a][:],
+                in_=grp[b][a][:].rearrange("p t m j -> p (t m j)"),
+            )
+
+        def gather_words(a):
+            for s in range(HALVES):
+                cols = slice(s * BANK // STRIPE, (s + 1) * BANK // STRIPE)
+                nc.vector.tensor_copy(out=v_w[a][s][:], in_=tab_w[a][:].indirect(offs_t[:, cols]))
+
+        def open_banks():
+            return [psum.tile([P, BANK], F32, name=f"bank{i}", tag=f"bank{i}") for i in range(8)]
+
+        def first_product(banks, b, a, t):
+            rows = slice(t * P, (t + 1) * P)
+            for s in range(HALVES):
+                nc.tensor.matmul_mx(
+                    out=banks[HALVES * t + s][:],
+                    lhsT=w1_c[b][a][:, rows].bitcast(FP8X4),
+                    lhsT_scale=w1_s[b][a][:, rows],
+                    rhs=v_w[a][s][:].bitcast(FP4X4),
+                    rhs_scale=v_sc[a][:, s * BANK : (s + 1) * BANK],
+                    start=(a == 0),
+                    stop=(a == K_PASSES - 1),
+                )
+
+        def fetch_h(banks, b, t):
+            for s in range(HALVES):
+                nc.scalar.activation(
+                    out=h[b][t][:, s * BANK : (s + 1) * BANK],
+                    in_=banks[HALVES * t + s][:],
+                    func=ACT.Copy,
+                    scale=g1[:, b, t : t + 1],
+                )
+
+        def pick_pairs(b, t, j0, j1, diff):
+            cols = slice(j0 // STRIPE, j1 // STRIPE)
+            right = ring.tile([P, j1 - j0], F32, name="right", tag="right")
+            nc.vector.tensor_copy(out=right[:], in_=h[b][t][:].indirect(pos2_t[:, cols]))
+            nc.vector.tensor_tensor(
+                out=diff[:, t, :], in0=h[b][t][:].indirect(pos1_t[:, cols]), in1=right[:], op=ALU.subtract
+            )
+
+        def bound(diff, c0, c1, name):
+            th = keep.tile([P, c1 - c0, PACK], F32, name=name, tag=name)
+            nc.scalar.activation(
+                out=th[:].rearrange("p (c i) t -> p c t i", i=PACK),
+                in_=diff[:, :, c0:c1].rearrange("p t (c i) -> p c t i", i=PACK),
+                func=ACT.Tanh,
+            )
+            return th
+
+        def make_z(b, th, name):
+            n = th.shape[1]
+            z = keep.tile([P, n, PACK], BF16, name=name + "_z", align_bytes=64)
+            codes = keep.tile([P, n], U32, name=name + "_c", align_bytes=64)
+            scales = keep.tile([P, n], U8, name=name + "_s", align_bytes=64)
+            nc.vector.tensor_tensor(
+                out=z[:], in0=th[:], in1=g2[:, b, :].unsqueeze(1).to_broadcast([P, n, PACK]), op=ALU.mult
+            )
+            nc.vector.quantize_mx(out=codes[:].bitcast(FP8X4), scales=scales[:], in_=z[:].rearrange("p n t -> p (n t)"))
+            return codes, scales
+
+        nc.vector.tensor_copy(out=v_sc[0][:], in_=tab_sc[:].indirect(offs_t[:]))
+        for a in range(1, K_PASSES):
+            for q in range(QUADS):
+                queue = nc.sync if a == 1 else nc.gpsimd
+                queue.dma_start(
+                    out=v_sc[a][32 * q : 32 * q + 4, :].bitcast(I32),
+                    in_=v_sc[0][32 * q + 4 * a : 32 * q + 4 * a + 4, :].bitcast(I32),
+                )
+        banks0 = open_banks()
+        for a in range(K_PASSES):
+            gather_words(a)
+            if a < K_PASSES - 1:
+                round_w1(0, a, 0, P, False)
+            else:
+                round_w1(0, a, 0, 48, False)
+                round_w1(0, a, 48, P, True)
+            load_w1(1, a)
+            quantize_w1(0, a)
+            for t in range(PACK):
+                first_product(banks0, 0, a, t)
+        round_w1(1, 0, 0, P, True)
+        w2_w = stage.tile([P, R_PASSES, 2 * N], U8, name="w2_w", tag="stage", align_bytes=64)
+        nc.sync.dma_start(out=w2_w[:].bitcast(I32), in_=w2_words.rearrange("a p c -> p a c").bitcast(I32))
+        quantize_w1(1, 0)
+
+        diff0 = keep.tile([P, PACK, PAIRS], F32, name="diff0")
+        banks1 = open_banks()
+        for t in range(PACK):
+            fetch_h(banks0, 0, t)
+            pick_pairs(0, t, 0, PAIRS, diff0)
+            if t in (1, 2):
+                round_w1(1, t, 0, P, False)
+                quantize_w1(1, t)
+        for t in range(PACK):
+            for a in range(K_PASSES):
+                first_product(banks1, 1, a, t)
+
+        parts = [(0, 256), (256, 384), (384, 512)]
+        diff_a = keep.tile([P, PACK, 256], F32, name="diff_a")
+        for t in range(PACK):
+            fetch_h(banks1, 1, t)
+            pick_pairs(1, t, 0, 256, diff_a)
+
+        z0 = []
+        for c in range(2):
+            th = bound(diff0, 256 * c, 256 * (c + 1), f"th0_{c}")
+            z0.append(make_z(0, th, f"z0_{c}"))
+
+        banks2 = open_banks()
+        out_v = out.rearrange("(i p) j -> p i j", p=P)
+
+        def second_product(part, b, z):
+            j0, j1 = parts[part]
+            n = j1 - j0
+            per_bank = 2 if n == 256 else 3
+            first_bank = [0, 3, 5][part]
+            codes, scales, c0 = z
+            for i in range(N_TILES):
+                bank = banks2[first_bank + i // per_bank]
+                for u in range(n // P):
+                    at = (i % per_bank) * n + u * P
+                    nc.tensor.matmul_mx(
+                        out=bank[:, at : at + P],
+                        lhsT=w2_w[:, b, 2 * P * i : 2 * P * (i + 1)].bitcast(FP4X4),
+                        lhsT_scale=w2_s[:, b, P * i : P * (i + 1)],
+                        rhs=codes[:, c0 + u * P : c0 + (u + 1) * P].bitcast(FP8X4),
+                        rhs_scale=scales[:, c0 + u * P : c0 + (u + 1) * P],
+                        start=(b == 0 and i % per_bank == 0 and u == 0),
+                        stop=(b == 1 and i % per_bank == per_bank - 1 and u == n // P - 1),
+                    )
+
+        def store(part):
+            j0, j1 = parts[part]
+            n = j1 - j0
+            per_bank = 2 if n == 256 else 3
+            first_bank = [0, 3, 5][part]
+            for c in range(N_TILES // per_bank):
+                res = keep.tile([P, per_bank, n], F32, name=f"res{part}_{c}")
+                src = banks2[first_bank + c][:, 0 : per_bank * n]
+                dst = res[:].rearrange("p i j -> p (i j)")
+                if part == 2 and c == 1:
+                    nc.vector.tensor_copy(out=dst, in_=src)
+                else:
+                    nc.scalar.copy(out=dst, in_=src)
+                nc.sync.dma_start(out=out_v[:, c * per_bank : (c + 1) * per_bank, j0:j1], in_=res[:])
+
+        second_product(0, 0, (z0[0][0], z0[0][1], 0))
+        second_product(1, 0, (z0[1][0], z0[1][1], 0))
+        second_product(2, 0, (z0[1][0], z0[1][1], P))
+
+        th_a = bound(diff_a, 0, 256, "th_a")
+        diff_b = keep.tile([P, PACK, P], F32, name="diff_b", tag="th0_1")
+        for t in range(PACK):
+            pick_pairs(1, t, 256, 384, diff_b)
+        z_a = make_z(1, th_a, "z_a")
+        second_product(0, 1, (z_a[0], z_a[1], 0))
+        th_b = bound(diff_b, 0, P, "th_b")
+        diff_c = keep.tile([P, PACK, P], F32, name="diff_c", tag="th_a")
+        for t in range(PACK):
+            pick_pairs(1, t, 384, 512, diff_c)
+        store(0)
+        z_b = make_z(1, th_b, "z_b")
+        second_product(1, 1, (z_b[0], z_b[1], 0))
+        th_c = bound(diff_c, 0, P, "th_c")
+        z_c = make_z(1, th_c, "z_c")
+        store(1)
+        second_product(2, 1, (z_c[0], z_c[1], 0))
+        store(2)

@@ -26,6 +26,8 @@ HALVES = S // BANK
 N_TILES = N // P
 STRIPE = 16
 QUADS = 4
+QUAD = 32
+MOVES = [(0, 64), (64, 68), (96, 100)]
 
 
 def tile_list_glyph_kerning_features_kernel(
@@ -33,83 +35,65 @@ def tile_list_glyph_kerning_features_kernel(
 ):
     nc = tc.nc
     with ExitStack() as ctx:
+        lists = ctx.enter_context(tc.tile_pool(name="lists", bufs=1))
         keep = ctx.enter_context(tc.tile_pool(name="keep", bufs=1))
-        stage = ctx.enter_context(tc.tile_pool(name="stage", bufs=K_PASSES))
-        ring = ctx.enter_context(tc.tile_pool(name="ring", bufs=2))
         psum = ctx.enter_context(tc.psum_pool(name="psum", bufs=1))
 
-        offs_t = keep.tile([P, S // STRIPE], U16, name="offs_t")
-        pos1_t = keep.tile([P, PAIRS // STRIPE], U16, name="pos1_t")
-        pos2_t = keep.tile([P, PAIRS // STRIPE], U16, name="pos2_t")
-        tab_sc = keep.tile([P, T], U8, name="tab_sc", align_bytes=64)
-        tab_w = [keep.tile([P, T], U16, name=f"tab_w{a}", align_bytes=64) for a in range(K_PASSES)]
-        v_sc = [keep.tile([P, S], U8, name=f"v_sc{a}", align_bytes=64) for a in range(K_PASSES)]
-        v_w = [
-            [keep.tile([P, BANK], U16, name=f"v_w{a}_{s}", align_bytes=64) for s in range(HALVES)]
-            for a in range(K_PASSES)
-        ]
-        raw = {}
-        grp = [
-            [keep.tile([P, PACK, P, PACK], BF16, name=f"grp{b}_{a}", align_bytes=64) for a in range(K_PASSES)]
-            for b in range(R_PASSES)
-        ]
-        w1_c = [
-            [keep.tile([P, PASS], U32, name=f"w1_c{b}_{a}", align_bytes=64) for a in range(K_PASSES)]
-            for b in range(R_PASSES)
-        ]
-        w1_s = [
-            [keep.tile([P, PASS], U8, name=f"w1_s{b}_{a}", align_bytes=64) for a in range(K_PASSES)]
-            for b in range(R_PASSES)
-        ]
-        h = [[keep.tile([P, S], F32, name=f"h{b}_{t}") for t in range(PACK)] for b in range(R_PASSES)]
-        g1 = keep.tile([P, R_PASSES, PACK], F32, name="g1")
-        g2 = keep.tile([P, R_PASSES, PACK], F32, name="g2")
-        w2_s = keep.tile([P, R_PASSES, N], U8, name="w2_s", align_bytes=64)
+        def tile(shape, dtype, name, slot=None):
+            return keep.tile(shape, dtype, name=name, tag=slot or name, align_bytes=64)
 
-        nc.vector.memset(tab_sc[:].bitcast(I32), 0)
-        for a in range(1, K_PASSES):
-            nc.vector.memset(v_sc[a][:].bitcast(I32), 0)
-        nc.vector.memset(w2_s[:].rearrange("p a c -> p (a c)").bitcast(I32), 0)
+        offs_t = lists.tile([P, S // STRIPE], U16, name="offs_t")
+        pos1_t = lists.tile([P, PAIRS // STRIPE], U16, name="pos1_t")
+        pos2_t = lists.tile([P, PAIRS // STRIPE], U16, name="pos2_t")
+        tab_sc = tile([P, T], U8, "tab_sc")
+        picked_sc = tile([P, S], U8, "picked_sc")
+        moved_sc = tile([P, K_PASSES - 1, S], U8, "moved_sc")
+        v_sc = [picked_sc[:]] + [moved_sc[:, a - 1, :] for a in range(1, K_PASSES)]
+        tab_w = {}
+        v_w = [[tile([P, BANK], U16, f"v_w{a}_{s}") for s in range(HALVES)] for a in range(K_PASSES)]
+        grp = {}
+        w1_c = {}
+        w1_s = [tile([P, K_PASSES * PASS], U8, f"w1_s{b}") for b in range(R_PASSES)]
+        h = [[tile([P, S], F32, f"h{b}_{t}") for t in range(PACK)] for b in range(R_PASSES)]
+        g1 = tile([P, R_PASSES, PACK], F32, "gain1_t")
+        g2 = tile([P, R_PASSES, PACK], F32, "gain2_t")
 
-        def load_w1(b, a):
+        nc.gpsimd.memset(tab_sc[:].bitcast(I32), 0)
+        nc.vector.memset(moved_sc[2 * QUAD :, :, :].rearrange("p a s -> p (a s)").bitcast(I32), 0)
+
+        def load_w1(b, a, slot):
             rows = w1[a * PASS : (a + 1) * PASS, b * PASS : (b + 1) * PASS]
-            raw[b, a] = stage.tile([P, PACK, PASS], F32, name=f"raw{b}_{a}", tag="stage", align_bytes=64)
-            nc.sync.dma_start(out=raw[b, a][:], in_=rows.rearrange("(p j) c -> p j c", j=PACK))
+            raw = tile([P, PACK, PASS], F32, f"raw{b}_{a}", slot)
+            nc.sync.dma_start(out=raw[:], in_=rows.rearrange("(p j) c -> p j c", j=PACK))
+            return raw
 
-        nc.sync.dma_start(offs_t[:], offs)
-        for q in range(QUADS):
-            nc.sync.dma_start(
-                out=tab_sc[32 * q : 32 * q + 4 * K_PASSES, :].bitcast(I32),
-                in_=tab_scales[:, 4 * q : 4 * q + 4, :].bitcast(I32),
-            )
-        for a in range(K_PASSES):
+        def load_words(a, slot=None):
+            tab_w[a] = tile([P, T], U16, f"tab_w{a}", slot)
             nc.sync.dma_start(out=tab_w[a][:].bitcast(I32), in_=tab_words[a].bitcast(I32))
-            load_w1(0, a)
-            if a == 1:
-                nc.sync.dma_start(out=g1[:], in_=gain1.rearrange("(b p t) -> p b t", b=R_PASSES, t=PACK))
-                nc.sync.dma_start(pos2_t[:], pos2)
-                nc.sync.dma_start(pos1_t[:], pos1)
-        nc.gpsimd.dma_start(out=g2[:], in_=gain2.rearrange("(b p t) -> p b t", b=R_PASSES, t=PACK))
-        for q in range(QUADS):
-            nc.gpsimd.dma_start(
-                out=w2_s[32 * q : 32 * q + 4, :, :].bitcast(I32),
-                in_=w2_scales[:, 4 * q : 4 * q + 4, :].rearrange("a r c -> r a c").bitcast(I32),
-            )
 
-        def round_w1(b, a, m0, m1, on_vector):
-            src = raw[b, a][:].rearrange("p j (m t) -> p m j t", t=PACK)[:, m0:m1]
-            dst = grp[b][a][:].rearrange("p t m j -> p m j t")[:, m0:m1]
+        def round_w1(raw, b, a, t0, t1, on_vector, slot=None):
+            rounded = tile([P, t1 - t0, P, PACK], BF16, f"grp{b}_{a}_{t0}", slot)
+            for t in range(t0, t1):
+                grp[b, a, t] = (rounded, t - t0)
+            src = raw[:].rearrange("p j (m t) -> p m j t", t=PACK)[:, :, :, t0:t1]
+            dst = rounded[:].rearrange("p t m j -> p m j t")
             if on_vector:
                 nc.vector.tensor_copy(out=dst, in_=src)
             else:
                 nc.scalar.activation(out=dst, in_=src, func=ACT.Copy)
 
-        def quantize_w1(b, a):
-            nc.vector.quantize_mx(
-                out=w1_c[b][a][:].bitcast(FP8X4),
-                scales=w1_s[b][a][:],
-                in_=grp[b][a][:].rearrange("p t m j -> p (t m j)"),
-            )
+        def quantize_w1(b, a, runs, slot=None):
+            first, last = runs[0][0], runs[-1][1]
+            codes = tile([P, (last - first) * P], U32, f"w1_c{b}_{a}_{first}", slot)
+            for t0, t1 in runs:
+                rounded, at = grp[b, a, t0]
+                nc.vector.quantize_mx(
+                    out=codes[:, (t0 - first) * P : (t1 - first) * P].bitcast(FP8X4),
+                    scales=w1_s[b][:, a * PASS + t0 * P : a * PASS + t1 * P],
+                    in_=rounded[:, at : at + t1 - t0].rearrange("p t m j -> p (t m j)"),
+                )
+            for t in range(first, last):
+                w1_c[b, a, t] = codes[:, (t - first) * P : (t - first + 1) * P]
 
         def gather_words(a):
             for s in range(HALVES):
@@ -119,18 +103,19 @@ def tile_list_glyph_kerning_features_kernel(
         def open_banks():
             return [psum.tile([P, BANK], F32, name=f"bank{i}", tag=f"bank{i}") for i in range(8)]
 
-        def first_product(banks, b, a, t):
-            rows = slice(t * P, (t + 1) * P)
-            for s in range(HALVES):
-                nc.tensor.matmul_mx(
-                    out=banks[HALVES * t + s][:],
-                    lhsT=w1_c[b][a][:, rows].bitcast(FP8X4),
-                    lhsT_scale=w1_s[b][a][:, rows],
-                    rhs=v_w[a][s][:].bitcast(FP4X4),
-                    rhs_scale=v_sc[a][:, s * BANK : (s + 1) * BANK],
-                    start=(a == 0),
-                    stop=(a == K_PASSES - 1),
-                )
+        def first_product(banks, b):
+            for t in range(PACK):
+                for a in range(K_PASSES):
+                    for s in range(HALVES):
+                        nc.tensor.matmul_mx(
+                            out=banks[HALVES * t + s][:],
+                            lhsT=w1_c[b, a, t].bitcast(FP8X4),
+                            lhsT_scale=w1_s[b][:, a * PASS + t * P : a * PASS + (t + 1) * P],
+                            rhs=v_w[a][s][:].bitcast(FP4X4),
+                            rhs_scale=v_sc[a][:, s * BANK : (s + 1) * BANK],
+                            start=(a == 0),
+                            stop=(a == K_PASSES - 1),
+                        )
 
         def fetch_h(banks, b, t):
             for s in range(HALVES):
@@ -141,16 +126,33 @@ def tile_list_glyph_kerning_features_kernel(
                     scale=g1[:, b, t : t + 1],
                 )
 
-        def pick_pairs(b, t, j0, j1, diff):
-            cols = slice(j0 // STRIPE, j1 // STRIPE)
-            right = ring.tile([P, j1 - j0], F32, name="right", tag="right")
-            nc.vector.tensor_copy(out=right[:], in_=h[b][t][:].indirect(pos2_t[:, cols]))
-            nc.vector.tensor_tensor(
-                out=diff[:, t, :], in0=h[b][t][:].indirect(pos1_t[:, cols]), in1=right[:], op=ALU.subtract
-            )
+        def pick_right(b, pieces, width, slot):
+            right = tile([P, width], F32, f"right{b}_{pieces[0][0]}_{pieces[0][1]}", slot)
+            at = 0
+            for t, j0, j1 in pieces:
+                cols = slice(j0 // STRIPE, j1 // STRIPE)
+                nc.vector.tensor_copy(out=right[:, at : at + j1 - j0], in_=h[b][t][:].indirect(pos2_t[:, cols]))
+                at = at + j1 - j0
+            return right
 
-        def bound(diff, c0, c1, name):
-            th = keep.tile([P, c1 - c0, PACK], F32, name=name, tag=name)
+        def pick_left(b, pieces, right, diff, first):
+            at = 0
+            for t, j0, j1 in pieces:
+                cols = slice(j0 // STRIPE, j1 // STRIPE)
+                nc.vector.tensor_tensor(
+                    out=diff[:, t, j0 - first : j1 - first],
+                    in0=h[b][t][:].indirect(pos1_t[:, cols]),
+                    in1=right[:, at : at + j1 - j0],
+                    op=ALU.subtract,
+                )
+                at = at + j1 - j0
+
+        def pick_pairs(b, t, j0, j1, diff, slot):
+            pieces = [(t, j0, j0 + 256), (t, j0 + 256, j1)]
+            pick_left(b, pieces, pick_right(b, pieces, j1 - j0, slot), diff, j0)
+
+        def bound(diff, c0, c1, name, slot=None):
+            th = tile([P, c1 - c0, PACK], F32, name, slot)
             nc.scalar.activation(
                 out=th[:].rearrange("p (c i) t -> p c t i", i=PACK),
                 in_=diff[:, :, c0:c1].rearrange("p t (c i) -> p c t i", i=PACK),
@@ -158,64 +160,95 @@ def tile_list_glyph_kerning_features_kernel(
             )
             return th
 
-        def make_z(b, th, name):
+        def apply_gain(b, th, z):
             n = th.shape[1]
-            z = keep.tile([P, n, PACK], BF16, name=name + "_z", align_bytes=64)
-            codes = keep.tile([P, n], U32, name=name + "_c", align_bytes=64)
-            scales = keep.tile([P, n], U8, name=name + "_s", align_bytes=64)
             nc.vector.tensor_tensor(
-                out=z[:], in0=th[:], in1=g2[:, b, :].unsqueeze(1).to_broadcast([P, n, PACK]), op=ALU.mult
+                out=z, in0=th[:], in1=g2[:, b, :].unsqueeze(1).to_broadcast([P, n, PACK]), op=ALU.mult
             )
+
+        def quantize_z(z, name):
+            n = z.shape[1]
+            codes = tile([P, n], U32, name + "_c")
+            scales = tile([P, n], U8, name + "_s")
             nc.vector.quantize_mx(out=codes[:].bitcast(FP8X4), scales=scales[:], in_=z[:].rearrange("p n t -> p (n t)"))
             return codes, scales
 
-        nc.vector.tensor_copy(out=v_sc[0][:], in_=tab_sc[:].indirect(offs_t[:]))
+        nc.gpsimd.dma_start(out=g1[:], in_=gain1.rearrange("(b p t) -> p b t", b=R_PASSES, t=PACK))
+        nc.gpsimd.dma_start(out=g2[:], in_=gain2.rearrange("(b p t) -> p b t", b=R_PASSES, t=PACK))
+        for q in range(QUADS):
+            nc.scalar.dma_start(
+                out=tab_sc[QUAD * q : QUAD * q + 4 * K_PASSES, :].bitcast(I32),
+                in_=tab_scales[:, 4 * q : 4 * q + 4, :].bitcast(I32),
+            )
+        nc.sync.dma_start(offs_t[:], offs)
+        load_words(0)
+        load_words(1)
+        w00 = load_w1(0, 0, "raw_even")
+        nc.sync.dma_start(pos2_t[:], pos2)
+        nc.sync.dma_start(pos1_t[:], pos1)
+        w01 = load_w1(0, 1, "raw_odd")
+
+        gather_words(0)
+        load_words(2, "tab_w0")
+        gather_words(1)
+        w02 = load_w1(0, 2, "tab_w1")
+        nc.vector.tensor_copy(out=picked_sc[:], in_=tab_sc[:].indirect(offs_t[:]))
         for a in range(1, K_PASSES):
-            for q in range(QUADS):
-                queue = nc.sync if a == 1 else nc.gpsimd
-                queue.dma_start(
-                    out=v_sc[a][32 * q : 32 * q + 4, :].bitcast(I32),
-                    in_=v_sc[0][32 * q + 4 * a : 32 * q + 4 * a + 4, :].bitcast(I32),
+            for r0, r1 in MOVES:
+                nc.sync.dma_start(
+                    out=moved_sc[r0:r1, a - 1, :].bitcast(I32),
+                    in_=picked_sc[r0 + 4 * a : r1 + 4 * a, :].bitcast(I32),
                 )
+        w10 = load_w1(1, 0, "tab_sc")
+        round_w1(w00, 0, 0, 0, PACK, False)
+        quantize_w1(0, 0, [(0, PACK)])
+        round_w1(w01, 0, 1, 0, PACK, False)
+        w11 = load_w1(1, 1, "raw_odd")
+        gather_words(2)
+        quantize_w1(0, 1, [(0, 1)])
+        round_w1(w02, 0, 2, 0, 1, True)
+        round_w1(w02, 0, 2, 1, PACK, False)
+        w12 = load_w1(1, 2, "tab_w1")
+        quantize_w1(0, 2, [(0, 1)])
+        quantize_w1(0, 1, [(1, 2), (2, PACK)], "grp0_2_0")
+        quantize_w1(0, 2, [(1, 2), (2, PACK)])
         banks0 = open_banks()
+        first_product(banks0, 0)
+        w2_s = w1_s[0][:].rearrange("p (b c) -> p b c", b=R_PASSES)
+        for q in range(QUADS):
+            nc.sync.dma_start(
+                out=w2_s[QUAD * q : QUAD * q + 4, :, :].bitcast(I32),
+                in_=w2_scales[:, 4 * q : 4 * q + 4, :].rearrange("a r c -> r a c").bitcast(I32),
+            )
+
+        diff0 = tile([P, PACK, PAIRS], F32, "diff0")
+        fetch_h(banks0, 0, 0)
+        pick_pairs(0, 0, 0, PAIRS, diff0, "right_even")
+        fetch_h(banks0, 0, 1)
+        pick_pairs(0, 1, 0, PAIRS, diff0, "right_odd")
         for a in range(K_PASSES):
-            gather_words(a)
-            if a < K_PASSES - 1:
-                round_w1(0, a, 0, P, False)
-            else:
-                round_w1(0, a, 0, 48, False)
-                round_w1(0, a, 48, P, True)
-            load_w1(1, a)
-            quantize_w1(0, a)
-            for t in range(PACK):
-                first_product(banks0, 0, a, t)
-        round_w1(1, 0, 0, P, True)
-        w2_w = stage.tile([P, R_PASSES, 2 * N], U8, name="w2_w", tag="stage", align_bytes=64)
+            slot = ["w1_c0_2_1", "grp1_1_0", "grp1_2_0"][a]
+            round_w1([w10, w11, w12][a], 1, a, 0, PACK, False, slot)
+            quantize_w1(1, a, [(0, PACK)])
+            if a + 2 < PACK:
+                fetch_h(banks0, 0, a + 2)
+                pick_pairs(0, a + 2, 0, PAIRS, diff0, slot)
+        w2_w = tile([P, R_PASSES, 2 * N], U8, "w2_w", "tab_sc")
         nc.sync.dma_start(out=w2_w[:].bitcast(I32), in_=w2_words.rearrange("a p c -> p a c").bitcast(I32))
-        quantize_w1(1, 0)
-
-        diff0 = keep.tile([P, PACK, PAIRS], F32, name="diff0")
         banks1 = open_banks()
-        for t in range(PACK):
-            fetch_h(banks0, 0, t)
-            pick_pairs(0, t, 0, PAIRS, diff0)
-            if t in (1, 2):
-                round_w1(1, t, 0, P, False)
-                quantize_w1(1, t)
-        for t in range(PACK):
-            for a in range(K_PASSES):
-                first_product(banks1, 1, a, t)
+        first_product(banks1, 1)
 
-        parts = [(0, 256), (256, 384), (384, 512)]
-        diff_a = keep.tile([P, PACK, 256], F32, name="diff_a")
-        for t in range(PACK):
-            fetch_h(banks1, 1, t)
-            pick_pairs(1, t, 0, 256, diff_a)
-
-        z0 = []
+        z0 = tile([P, PAIRS, PACK], BF16, "z0")
         for c in range(2):
             th = bound(diff0, 256 * c, 256 * (c + 1), f"th0_{c}")
-            z0.append(make_z(0, th, f"z0_{c}"))
+            apply_gain(0, th, z0[:, 256 * c : 256 * (c + 1), :])
+        q0 = quantize_z(z0, "q0")
+
+        parts = [(0, 256), (256, 384), (384, 512)]
+        diff_ab = tile([P, PACK, 384], F32, "diff_ab")
+        for t in range(PACK):
+            fetch_h(banks1, 1, t)
+            pick_pairs(1, t, 0, 384, diff_ab, ["right_even", "right_odd"][t % 2])
 
         banks2 = open_banks()
         out_v = out.rearrange("(i p) j -> p i j", p=P)
@@ -240,13 +273,13 @@ def tile_list_glyph_kerning_features_kernel(
                         stop=(b == 1 and i % per_bank == per_bank - 1 and u == n // P - 1),
                     )
 
-        def store(part):
+        def store(part, which):
             j0, j1 = parts[part]
             n = j1 - j0
             per_bank = 2 if n == 256 else 3
             first_bank = [0, 3, 5][part]
-            for c in range(N_TILES // per_bank):
-                res = keep.tile([P, per_bank, n], F32, name=f"res{part}_{c}")
+            for c in which:
+                res = tile([P, per_bank, n], F32, f"res{part}_{c}")
                 src = banks2[first_bank + c][:, 0 : per_bank * n]
                 dst = res[:].rearrange("p i j -> p (i j)")
                 if part == 2 and c == 1:
@@ -255,25 +288,31 @@ def tile_list_glyph_kerning_features_kernel(
                     nc.scalar.copy(out=dst, in_=src)
                 nc.sync.dma_start(out=out_v[:, c * per_bank : (c + 1) * per_bank, j0:j1], in_=res[:])
 
-        second_product(0, 0, (z0[0][0], z0[0][1], 0))
-        second_product(1, 0, (z0[1][0], z0[1][1], 0))
-        second_product(2, 0, (z0[1][0], z0[1][1], P))
+        for part in range(3):
+            second_product(part, 0, (q0[0], q0[1], parts[part][0]))
 
-        th_a = bound(diff_a, 0, 256, "th_a")
-        diff_b = keep.tile([P, PACK, P], F32, name="diff_b", tag="th0_1")
-        for t in range(PACK):
-            pick_pairs(1, t, 256, 384, diff_b)
-        z_a = make_z(1, th_a, "z_a")
-        second_product(0, 1, (z_a[0], z_a[1], 0))
-        th_b = bound(diff_b, 0, P, "th_b")
-        diff_c = keep.tile([P, PACK, P], F32, name="diff_c", tag="th_a")
-        for t in range(PACK):
-            pick_pairs(1, t, 384, 512, diff_c)
-        store(0)
-        z_b = make_z(1, th_b, "z_b")
-        second_product(1, 1, (z_b[0], z_b[1], 0))
+        diff_c = tile([P, PACK, P], F32, "diff_c")
+        early = [(0, 384, 512), (1, 384, 512)]
+        late = [(2, 384, 512), (3, 384, 512)]
+        pick_left(1, early, pick_right(1, early, 256, "right_odd"), diff_c, 384)
+        th_a = bound(diff_ab, 0, 256, "th_a")
+        th_b = bound(diff_ab, 256, 384, "th_b")
+        z_a = tile([P, 256, PACK], BF16, "z_a")
+        apply_gain(1, th_a, z_a[:])
+        right_late = pick_right(1, late, 256, "th_a")
+        q_a = quantize_z(z_a, "q_a")
+        second_product(0, 1, (q_a[0], q_a[1], 0))
+        pick_left(1, late, right_late, diff_c, 384)
+        store(0, (0,))
         th_c = bound(diff_c, 0, P, "th_c")
-        z_c = make_z(1, th_c, "z_c")
-        store(1)
-        second_product(2, 1, (z_c[0], z_c[1], 0))
-        store(2)
+        store(0, (1, 2))
+        z_b = tile([P, P, PACK], BF16, "z_b", "th_a")
+        apply_gain(1, th_b, z_b[:])
+        q_b = quantize_z(z_b, "q_b")
+        second_product(1, 1, (q_b[0], q_b[1], 0))
+        z_c = tile([P, P, PACK], BF16, "z_c")
+        apply_gain(1, th_c, z_c[:])
+        q_c = quantize_z(z_c, "q_c")
+        store(1, (0, 1))
+        second_product(2, 1, (q_c[0], q_c[1], 0))
+        store(2, (0, 1))

@@ -55,15 +55,13 @@ def tile_list_glyph_kerning_features_kernel(
         w1_c = {}
         w1_s = [tile([P, K_PASSES * PASS], U8, f"w1_s{b}") for b in range(R_PASSES)]
         h = [[tile([P, S], F32, f"h{b}_{t}") for t in range(PACK)] for b in range(R_PASSES)]
-        g1 = tile([P, R_PASSES, PACK], F32, "gain1_t")
-        g2 = tile([P, R_PASSES, PACK], F32, "gain2_t")
 
         nc.gpsimd.memset(tab_sc[:].bitcast(I32), 0)
         nc.vector.memset(moved_sc[2 * QUAD :, :, :].rearrange("p a s -> p (a s)").bitcast(I32), 0)
 
-        def load_w1(b, a, slot):
-            rows = w1[a * PASS : (a + 1) * PASS, b * PASS : (b + 1) * PASS]
-            raw = tile([P, PACK, PASS], F32, f"raw{b}_{a}", slot)
+        def load_w1(b, a, slot, m0=0, m1=P):
+            rows = w1[a * PASS : (a + 1) * PASS, b * PASS + PACK * m0 : b * PASS + PACK * m1]
+            raw = tile([P, PACK, PACK * (m1 - m0)], F32, f"raw{b}_{a}_{m0}", slot)
             nc.sync.dma_start(out=raw[:], in_=rows.rearrange("(p j) c -> p j c", j=PACK))
             return raw
 
@@ -71,16 +69,21 @@ def tile_list_glyph_kerning_features_kernel(
             tab_w[a] = tile([P, T], U16, f"tab_w{a}", slot)
             nc.sync.dma_start(out=tab_w[a][:].bitcast(I32), in_=tab_words[a].bitcast(I32))
 
-        def round_w1(raw, b, a, t0, t1, on_vector, slot=None):
-            rounded = tile([P, t1 - t0, P, PACK], BF16, f"grp{b}_{a}_{t0}", slot)
+        def rounded_tile(b, a, t0, t1):
+            rounded = tile([P, t1 - t0, P, PACK], BF16, f"grp{b}_{a}_{t0}")
             for t in range(t0, t1):
                 grp[b, a, t] = (rounded, t - t0)
-            src = raw[:].rearrange("p j (m t) -> p m j t", t=PACK)[:, :, :, t0:t1]
-            dst = rounded[:].rearrange("p t m j -> p m j t")
+            return rounded[:].rearrange("p t m j -> p m j t")
+
+        def round_into(dst, src, on_vector):
             if on_vector:
                 nc.vector.tensor_copy(out=dst, in_=src)
             else:
                 nc.scalar.activation(out=dst, in_=src, func=ACT.Copy)
+
+        def round_w1(raw, b, a, t0, t1, on_vector):
+            src = raw[:].rearrange("p j (m t) -> p m j t", t=PACK)[:, :, :, t0:t1]
+            round_into(rounded_tile(b, a, t0, t1), src, on_vector)
 
         def quantize_w1(b, a, runs, slot=None):
             first, last = runs[0][0], runs[-1][1]
@@ -166,6 +169,22 @@ def tile_list_glyph_kerning_features_kernel(
                 out=z, in0=th[:], in1=g2[:, b, :].unsqueeze(1).to_broadcast([P, n, PACK]), op=ALU.mult
             )
 
+        def bound_rows(diff, t0, t1, name, pieces):
+            n = diff.shape[2]
+            th = tile([P, t1 - t0, n], F32, name)
+            nc.scalar.activation(out=th[:], in_=diff[:, t0:t1, :], func=ACT.Tanh)
+            for t in range(t0, t1):
+                for z_rows, c0, c1 in pieces:
+                    nc.scalar.activation(
+                        out=z_rows[:, t, :], in_=th[:, t - t0, c0:c1], func=ACT.Copy, scale=g2[:, 1, t : t + 1]
+                    )
+
+        def interleave(z_rows, z):
+            nc.vector.tensor_copy(
+                out=z[:].rearrange("p (c i) t -> p c t i", i=PACK),
+                in_=z_rows[:].rearrange("p t (c i) -> p c t i", i=PACK),
+            )
+
         def quantize_z(z, name):
             n = z.shape[1]
             codes = tile([P, n], U32, name + "_c")
@@ -173,8 +192,6 @@ def tile_list_glyph_kerning_features_kernel(
             nc.vector.quantize_mx(out=codes[:].bitcast(FP8X4), scales=scales[:], in_=z[:].rearrange("p n t -> p (n t)"))
             return codes, scales
 
-        nc.gpsimd.dma_start(out=g1[:], in_=gain1.rearrange("(b p t) -> p b t", b=R_PASSES, t=PACK))
-        nc.gpsimd.dma_start(out=g2[:], in_=gain2.rearrange("(b p t) -> p b t", b=R_PASSES, t=PACK))
         for q in range(QUADS):
             nc.scalar.dma_start(
                 out=tab_sc[QUAD * q : QUAD * q + 4 * K_PASSES, :].bitcast(I32),
@@ -193,25 +210,32 @@ def tile_list_glyph_kerning_features_kernel(
         gather_words(1)
         w02 = load_w1(0, 2, "tab_w1")
         nc.vector.tensor_copy(out=picked_sc[:], in_=tab_sc[:].indirect(offs_t[:]))
-        for a in range(1, K_PASSES):
+        for a in range(K_PASSES - 1, 0, -1):
             for r0, r1 in MOVES:
                 nc.sync.dma_start(
                     out=moved_sc[r0:r1, a - 1, :].bitcast(I32),
                     in_=picked_sc[r0 + 4 * a : r1 + 4 * a, :].bitcast(I32),
                 )
-        w10 = load_w1(1, 0, "tab_sc")
+        w10_low = load_w1(1, 0, "tab_sc", 0, P // 2)
         round_w1(w00, 0, 0, 0, PACK, False)
+        g1 = tile([P, R_PASSES, PACK], F32, "gain1_t", "raw_even")
+        nc.sync.dma_start(out=g1[:], in_=gain1.rearrange("(b p t) -> p b t", b=R_PASSES, t=PACK))
         quantize_w1(0, 0, [(0, PACK)])
         round_w1(w01, 0, 1, 0, PACK, False)
-        w11 = load_w1(1, 1, "raw_odd")
         gather_words(2)
+        w10_high = load_w1(1, 0, "tab_w0", P // 2, P)
         quantize_w1(0, 1, [(0, 1)])
         round_w1(w02, 0, 2, 0, 1, True)
         round_w1(w02, 0, 2, 1, PACK, False)
-        w12 = load_w1(1, 2, "tab_w1")
+        w11 = load_w1(1, 1, "tab_w1")
         quantize_w1(0, 2, [(0, 1)])
         quantize_w1(0, 1, [(1, 2), (2, PACK)], "grp0_2_0")
         quantize_w1(0, 2, [(1, 2), (2, PACK)])
+        g2 = tile([P, R_PASSES, PACK], F32, "gain2_t", "grp0_2_1")
+        nc.sync.dma_start(out=g2[:], in_=gain2.rearrange("(b p t) -> p b t", b=R_PASSES, t=PACK))
+        grp10 = rounded_tile(1, 0, 0, PACK)
+        round_into(grp10[:, 0 : P // 2], w10_low[:].rearrange("p j (m t) -> p m j t", t=PACK), True)
+        w12 = load_w1(1, 2, "tab_sc")
         banks0 = open_banks()
         first_product(banks0, 0)
         w2_s = w1_s[0][:].rearrange("p (b c) -> p b c", b=R_PASSES)
@@ -227,13 +251,15 @@ def tile_list_glyph_kerning_features_kernel(
         fetch_h(banks0, 0, 1)
         pick_pairs(0, 1, 0, PAIRS, diff0, "right_odd")
         for a in range(K_PASSES):
-            slot = ["w1_c0_2_1", "grp1_1_0", "grp1_2_0"][a]
-            round_w1([w10, w11, w12][a], 1, a, 0, PACK, False, slot)
+            if a == 0:
+                round_into(grp10[:, P // 2 : P], w10_high[:].rearrange("p j (m t) -> p m j t", t=PACK), False)
+            else:
+                round_w1([w11, w12][a - 1], 1, a, 0, PACK, False)
             quantize_w1(1, a, [(0, PACK)])
             if a + 2 < PACK:
                 fetch_h(banks0, 0, a + 2)
-                pick_pairs(0, a + 2, 0, PAIRS, diff0, slot)
-        w2_w = tile([P, R_PASSES, 2 * N], U8, "w2_w", "tab_sc")
+                pick_pairs(0, a + 2, 0, PAIRS, diff0, f"grp1_{a}_0")
+        w2_w = tile([P, R_PASSES, 2 * N], U8, "w2_w", "tab_w0")
         nc.sync.dma_start(out=w2_w[:].bitcast(I32), in_=w2_words.rearrange("a p c -> p a c").bitcast(I32))
         banks1 = open_banks()
         first_product(banks1, 1)
@@ -249,6 +275,12 @@ def tile_list_glyph_kerning_features_kernel(
         for t in range(PACK):
             fetch_h(banks1, 1, t)
             pick_pairs(1, t, 0, 384, diff_ab, ["right_even", "right_odd"][t % 2])
+
+        rows_a = tile([P, PACK, 256], BF16, "rows_a")
+        rows_b = tile([P, PACK, P], BF16, "rows_b")
+        rows_c = tile([P, PACK, P], BF16, "rows_c")
+        for t in range(PACK):
+            bound_rows(diff_ab, t, t + 1, f"th_ab{t}", [(rows_a, 0, 256), (rows_b, 256, 384)])
 
         banks2 = open_banks()
         out_v = out.rearrange("(i p) j -> p i j", p=P)
@@ -295,23 +327,23 @@ def tile_list_glyph_kerning_features_kernel(
         early = [(0, 384, 512), (1, 384, 512)]
         late = [(2, 384, 512), (3, 384, 512)]
         pick_left(1, early, pick_right(1, early, 256, "right_odd"), diff_c, 384)
-        th_a = bound(diff_ab, 0, 256, "th_a")
-        th_b = bound(diff_ab, 256, 384, "th_b")
+        bound_rows(diff_c, 0, 2, "th_c0", [(rows_c, 0, P)])
         z_a = tile([P, 256, PACK], BF16, "z_a")
-        apply_gain(1, th_a, z_a[:])
-        right_late = pick_right(1, late, 256, "th_a")
+        interleave(rows_a, z_a)
+        right_late = pick_right(1, late, 256, "rows_a")
         q_a = quantize_z(z_a, "q_a")
         second_product(0, 1, (q_a[0], q_a[1], 0))
         pick_left(1, late, right_late, diff_c, 384)
         store(0, (0,))
-        th_c = bound(diff_c, 0, P, "th_c")
+        for t in (2, 3):
+            bound_rows(diff_c, t, t + 1, f"th_c{t}", [(rows_c, 0, P)])
         store(0, (1, 2))
-        z_b = tile([P, P, PACK], BF16, "z_b", "th_a")
-        apply_gain(1, th_b, z_b[:])
+        z_b = tile([P, P, PACK], BF16, "z_b", "rows_a")
+        interleave(rows_b, z_b)
         q_b = quantize_z(z_b, "q_b")
         second_product(1, 1, (q_b[0], q_b[1], 0))
         z_c = tile([P, P, PACK], BF16, "z_c")
-        apply_gain(1, th_c, z_c[:])
+        interleave(rows_c, z_c)
         q_c = quantize_z(z_c, "q_c")
         store(1, (0, 1))
         second_product(2, 1, (q_c[0], q_c[1], 0))

from contextlib import ExitStack

import concourse.mybir as mybir

K, H, N, T, S, PAIRS = 1536, 1024, 768, 2048, 1024, 512
FLOPS = 2 * K * H * S + 2 * H * N * PAIRS

F32 = mybir.dt.float32
BF16 = mybir.dt.bfloat16
I32 = mybir.dt.int32
U32 = mybir.dt.uint32
U16 = mybir.dt.uint16
U8 = mybir.dt.uint8
FP8X4 = mybir.dt.float8_e4m3fn_x4
FP4X4 = mybir.dt.float4_e2m1fn_x4
ACT = mybir.ActivationFunctionType
ALU = mybir.AluOpType

P = 128
PACK = 4
PASS = P * PACK
K_PASSES = K // PASS
R_PASSES = H // PASS
BANK = 512
HALVES = S // BANK
N_TILES = N // P
STRIPE = 16
QUADS = 4
QUAD = 32
MOVES = [(0, 64), (64, 68), (96, 100)]


def tile_list_glyph_kerning_features_kernel(
    tc, tab_words, tab_scales, offs, pos1, pos2, w1, gain1, gain2, w2_words, w2_scales, out
):
    nc = tc.nc
    with ExitStack() as ctx:
        lists = ctx.enter_context(tc.tile_pool(name="lists", bufs=1))
        keep = ctx.enter_context(tc.tile_pool(name="keep", bufs=1))
        psum = ctx.enter_context(tc.psum_pool(name="psum", bufs=1))

        def tile(shape, dtype, name, slot=None):
            return keep.tile(shape, dtype, name=name, tag=slot or name, align_bytes=64)

        offs_t = lists.tile([P, S // STRIPE], U16, name="offs_t")
        pos1_t = lists.tile([P, PAIRS // STRIPE], U16, name="pos1_t")
        pos2_t = lists.tile([P, PAIRS // STRIPE], U16, name="pos2_t")
        tab_sc = tile([P, T], U8, "tab_sc")
        picked_sc = tile([P, S], U8, "picked_sc")
        moved_sc = tile([P, K_PASSES - 1, S], U8, "moved_sc")
        v_sc = [picked_sc[:]] + [moved_sc[:, a - 1, :] for a in range(1, K_PASSES)]
        tab_w = {}
        v_w = [[tile([P, BANK], U16, f"v_w{a}_{s}") for s in range(HALVES)] for a in range(K_PASSES)]
        grp = {}
        w1_c = {}
        w1_s = [tile([P, K_PASSES * PASS], U8, f"w1_s{b}") for b in range(R_PASSES)]
        h = [[tile([P, S], F32, f"h{b}_{t}") for t in range(PACK)] for b in range(R_PASSES)]

        nc.gpsimd.memset(tab_sc[:].bitcast(I32), 0)
        nc.vector.memset(moved_sc[2 * QUAD :, :, :].rearrange("p a s -> p (a s)").bitcast(I32), 0)

        def load_w1(b, a, slot, m0=0, m1=P):
            rows = w1[a * PASS : (a + 1) * PASS, b * PASS + PACK * m0 : b * PASS + PACK * m1]
            raw = tile([P, PACK, PACK * (m1 - m0)], F32, f"raw{b}_{a}_{m0}", slot)
            nc.sync.dma_start(out=raw[:], in_=rows.rearrange("(p j) c -> p j c", j=PACK))
            return raw

        def load_words(a, slot=None):
            tab_w[a] = tile([P, T], U16, f"tab_w{a}", slot)
            nc.sync.dma_start(out=tab_w[a][:].bitcast(I32), in_=tab_words[a].bitcast(I32))

        def rounded_tile(b, a, t0, t1):
            rounded = tile([P, t1 - t0, P, PACK], BF16, f"grp{b}_{a}_{t0}")
            for t in range(t0, t1):
                grp[b, a, t] = (rounded, t - t0)
            return rounded[:].rearrange("p t m j -> p m j t")

        def round_into(dst, src, on_vector):
            if on_vector:
                nc.vector.tensor_copy(out=dst, in_=src)
            else:
                nc.scalar.activation(out=dst, in_=src, func=ACT.Copy)

        def round_w1(raw, b, a, t0, t1, on_vector):
            src = raw[:].rearrange("p j (m t) -> p m j t", t=PACK)[:, :, :, t0:t1]
            round_into(rounded_tile(b, a, t0, t1), src, on_vector)

        def quantize_w1(b, a, runs, slot=None):
            first, last = runs[0][0], runs[-1][1]
            codes = tile([P, (last - first) * P], U32, f"w1_c{b}_{a}_{first}", slot)
            for t0, t1 in runs:
                rounded, at = grp[b, a, t0]
                nc.vector.quantize_mx(
                    out=codes[:, (t0 - first) * P : (t1 - first) * P].bitcast(FP8X4),
                    scales=w1_s[b][:, a * PASS + t0 * P : a * PASS + t1 * P],
                    in_=rounded[:, at : at + t1 - t0].rearrange("p t m j -> p (t m j)"),
                )
            for t in range(first, last):
                w1_c[b, a, t] = codes[:, (t - first) * P : (t - first + 1) * P]

        def gather_words(a):
            for s in range(HALVES):
                cols = slice(s * BANK // STRIPE, (s + 1) * BANK // STRIPE)
                nc.vector.tensor_copy(out=v_w[a][s][:], in_=tab_w[a][:].indirect(offs_t[:, cols]))

        def open_banks():
            return [psum.tile([P, BANK], F32, name=f"bank{i}", tag=f"bank{i}") for i in range(8)]

        def first_product(banks, b):
            for t in range(PACK):
                for a in range(K_PASSES):
                    for s in range(HALVES):
                        nc.tensor.matmul_mx(
                            out=banks[HALVES * t + s][:],
                            lhsT=w1_c[b, a, t].bitcast(FP8X4),
                            lhsT_scale=w1_s[b][:, a * PASS + t * P : a * PASS + (t + 1) * P],
                            rhs=v_w[a][s][:].bitcast(FP4X4),
                            rhs_scale=v_sc[a][:, s * BANK : (s + 1) * BANK],
                            start=(a == 0),
                            stop=(a == K_PASSES - 1),
                        )

        def fetch_h(banks, b, t):
            for s in range(HALVES):
                nc.scalar.activation(
                    out=h[b][t][:, s * BANK : (s + 1) * BANK],
                    in_=banks[HALVES * t + s][:],
                    func=ACT.Copy,
                    scale=g1[:, b, t : t + 1],
                )

        def pick_right(b, pieces, width, slot):
            right = tile([P, width], F32, f"right{b}_{pieces[0][0]}_{pieces[0][1]}", slot)
            at = 0
            for t, j0, j1 in pieces:
                cols = slice(j0 // STRIPE, j1 // STRIPE)
                nc.vector.tensor_copy(out=right[:, at : at + j1 - j0], in_=h[b][t][:].indirect(pos2_t[:, cols]))
                at = at + j1 - j0
            return right

        def pick_left(b, pieces, right, diff, first):
            at = 0
            for t, j0, j1 in pieces:
                cols = slice(j0 // STRIPE, j1 // STRIPE)
                nc.vector.tensor_tensor(
                    out=diff[:, t, j0 - first : j1 - first],
                    in0=h[b][t][:].indirect(pos1_t[:, cols]),
                    in1=right[:, at : at + j1 - j0],
                    op=ALU.subtract,
                )
                at = at + j1 - j0

        def pick_pairs(b, t, j0, j1, diff, slot):
            pieces = [(t, j0, j0 + 256), (t, j0 + 256, j1)]
            pick_left(b, pieces, pick_right(b, pieces, j1 - j0, slot), diff, j0)

        def bound(diff, c0, c1, name, slot=None):
            th = tile([P, c1 - c0, PACK], F32, name, slot)
            nc.scalar.activation(
                out=th[:].rearrange("p (c i) t -> p c t i", i=PACK),
                in_=diff[:, :, c0:c1].rearrange("p t (c i) -> p c t i", i=PACK),
                func=ACT.Tanh,
            )
            return th

        def apply_gain(b, th, z):
            n = th.shape[1]
            nc.vector.tensor_tensor(
                out=z, in0=th[:], in1=g2[:, b, :].unsqueeze(1).to_broadcast([P, n, PACK]), op=ALU.mult
            )

        def bound_rows(diff, t0, t1, name, pieces):
            n = diff.shape[2]
            th = tile([P, t1 - t0, n], F32, name)
            nc.scalar.activation(out=th[:], in_=diff[:, t0:t1, :], func=ACT.Tanh)
            for t in range(t0, t1):
                for z_rows, c0, c1 in pieces:
                    nc.scalar.activation(
                        out=z_rows[:, t, :], in_=th[:, t - t0, c0:c1], func=ACT.Copy, scale=g2[:, 1, t : t + 1]
                    )

        def interleave(z_rows, z):
            nc.vector.tensor_copy(
                out=z[:].rearrange("p (c i) t -> p c t i", i=PACK),
                in_=z_rows[:].rearrange("p t (c i) -> p c t i", i=PACK),
            )

        def quantize_z(z, name):
            n = z.shape[1]
            codes = tile([P, n], U32, name + "_c")
            scales = tile([P, n], U8, name + "_s")
            nc.vector.quantize_mx(out=codes[:].bitcast(FP8X4), scales=scales[:], in_=z[:].rearrange("p n t -> p (n t)"))
            return codes, scales

        for q in range(QUADS):
            nc.scalar.dma_start(
                out=tab_sc[QUAD * q : QUAD * q + 4 * K_PASSES, :].bitcast(I32),
                in_=tab_scales[:, 4 * q : 4 * q + 4, :].bitcast(I32),
            )
        nc.sync.dma_start(offs_t[:], offs)
        load_words(0)
        load_words(1)
        w00 = load_w1(0, 0, "raw_even")
        nc.sync.dma_start(pos2_t[:], pos2)
        nc.sync.dma_start(pos1_t[:], pos1)
        w01 = load_w1(0, 1, "raw_odd")

        gather_words(0)
        load_words(2, "tab_w0")
        gather_words(1)
        w02 = load_w1(0, 2, "tab_w1")
        nc.vector.tensor_copy(out=picked_sc[:], in_=tab_sc[:].indirect(offs_t[:]))
        for a in range(K_PASSES - 1, 0, -1):
            for r0, r1 in MOVES:
                nc.sync.dma_start(
                    out=moved_sc[r0:r1, a - 1, :].bitcast(I32),
                    in_=picked_sc[r0 + 4 * a : r1 + 4 * a, :].bitcast(I32),
                )
        w10_low = load_w1(1, 0, "tab_sc", 0, P // 2)
        round_w1(w00, 0, 0, 0, PACK, False)
        g1 = tile([P, R_PASSES, PACK], F32, "gain1_t", "raw_even")
        nc.sync.dma_start(out=g1[:], in_=gain1.rearrange("(b p t) -> p b t", b=R_PASSES, t=PACK))
        quantize_w1(0, 0, [(0, PACK)])
        round_w1(w01, 0, 1, 0, PACK, False)
        gather_words(2)
        w10_high = load_w1(1, 0, "tab_w0", P // 2, P)
        quantize_w1(0, 1, [(0, 1)])
        round_w1(w02, 0, 2, 0, 1, True)
        round_w1(w02, 0, 2, 1, PACK, False)
        w11 = load_w1(1, 1, "tab_w1")
        quantize_w1(0, 2, [(0, 1)])
        quantize_w1(0, 1, [(1, 2), (2, PACK)], "grp0_2_0")
        quantize_w1(0, 2, [(1, 2), (2, PACK)])
        g2 = tile([P, R_PASSES, PACK], F32, "gain2_t", "grp0_2_1")
        nc.sync.dma_start(out=g2[:], in_=gain2.rearrange("(b p t) -> p b t", b=R_PASSES, t=PACK))
        grp10 = rounded_tile(1, 0, 0, PACK)
        round_into(grp10[:, 0 : P // 2], w10_low[:].rearrange("p j (m t) -> p m j t", t=PACK), True)
        w12 = load_w1(1, 2, "tab_sc")
        banks0 = open_banks()
        first_product(banks0, 0)
        w2_s = w1_s[0][:].rearrange("p (b c) -> p b c", b=R_PASSES)
        for q in range(QUADS):
            nc.sync.dma_start(
                out=w2_s[QUAD * q : QUAD * q + 4, :, :].bitcast(I32),
                in_=w2_scales[:, 4 * q : 4 * q + 4, :].rearrange("a r c -> r a c").bitcast(I32),
            )

        diff0 = tile([P, PACK, PAIRS], F32, "diff0")
        fetch_h(banks0, 0, 0)
        pick_pairs(0, 0, 0, PAIRS, diff0, "right_even")
        fetch_h(banks0, 0, 1)
        pick_pairs(0, 1, 0, PAIRS, diff0, "right_odd")
        for a in range(K_PASSES):
            if a == 0:
                round_into(grp10[:, P // 2 : P], w10_high[:].rearrange("p j (m t) -> p m j t", t=PACK), False)
            else:
                round_w1([w11, w12][a - 1], 1, a, 0, PACK, False)
            quantize_w1(1, a, [(0, PACK)])
            if a + 2 < PACK:
                fetch_h(banks0, 0, a + 2)
                pick_pairs(0, a + 2, 0, PAIRS, diff0, f"grp1_{a}_0")
        w2_w = tile([P, R_PASSES, 2 * N], U8, "w2_w", "tab_w0")
        nc.sync.dma_start(out=w2_w[:].bitcast(I32), in_=w2_words.rearrange("a p c -> p a c").bitcast(I32))
        banks1 = open_banks()
        first_product(banks1, 1)

        z0 = tile([P, PAIRS, PACK], BF16, "z0")
        for c in range(2):
            th = bound(diff0, 256 * c, 256 * (c + 1), f"th0_{c}")
            apply_gain(0, th, z0[:, 256 * c : 256 * (c + 1), :])
        q0 = quantize_z(z0, "q0")

        parts = [(0, 256), (256, 384), (384, 512)]
        diff_ab = tile([P, PACK, 384], F32, "diff_ab")
        for t in range(PACK):
            fetch_h(banks1, 1, t)
            pick_pairs(1, t, 0, 384, diff_ab, ["right_even", "right_odd"][t % 2])

        rows_a = tile([P, PACK, 256], BF16, "rows_a")
        rows_b = tile([P, PACK, P], BF16, "rows_b")
        rows_c = tile([P, PACK, P], BF16, "rows_c")
        for t in range(PACK):
            bound_rows(diff_ab, t, t + 1, f"th_ab{t}", [(rows_a, 0, 256), (rows_b, 256, 384)])

        banks2 = open_banks()
        out_v = out.rearrange("(i p) j -> p i j", p=P)

        def second_product(part, b, z):
            j0, j1 = parts[part]
            n = j1 - j0
            per_bank = 2 if n == 256 else 3
            first_bank = [0, 3, 5][part]
            codes, scales, c0 = z
            for i in range(N_TILES):
                bank = banks2[first_bank + i // per_bank]
                for u in range(n // P):
                    at = (i % per_bank) * n + u * P
                    nc.tensor.matmul_mx(
                        out=bank[:, at : at + P],
                        lhsT=w2_w[:, b, 2 * P * i : 2 * P * (i + 1)].bitcast(FP4X4),
                        lhsT_scale=w2_s[:, b, P * i : P * (i + 1)],
                        rhs=codes[:, c0 + u * P : c0 + (u + 1) * P].bitcast(FP8X4),
                        rhs_scale=scales[:, c0 + u * P : c0 + (u + 1) * P],
                        start=(b == 0 and i % per_bank == 0 and u == 0),
                        stop=(b == 1 and i % per_bank == per_bank - 1 and u == n // P - 1),
                    )

        def store(part, which):
            j0, j1 = parts[part]
            n = j1 - j0
            per_bank = 2 if n == 256 else 3
            first_bank = [0, 3, 5][part]
            for c in which:
                res = tile([P, per_bank, n], F32, f"res{part}_{c}")
                src = banks2[first_bank + c][:, 0 : per_bank * n]
                dst = res[:].rearrange("p i j -> p (i j)")
                if part == 2 and c == 1:
                    nc.vector.tensor_copy(out=dst, in_=src)
                else:
                    nc.scalar.copy(out=dst, in_=src)
                nc.sync.dma_start(out=out_v[:, c * per_bank : (c + 1) * per_bank, j0:j1], in_=res[:])

        for part in range(3):
            second_product(part, 0, (q0[0], q0[1], parts[part][0]))

        diff_c = tile([P, PACK, P], F32, "diff_c")
        early = [(0, 384, 512), (1, 384, 512)]
        late = [(2, 384, 512), (3, 384, 512)]
        pick_left(1, early, pick_right(1, early, 256, "right_odd"), diff_c, 384)
        bound_rows(diff_c, 0, 2, "th_c0", [(rows_c, 0, P)])
        z_a = tile([P, 256, PACK], BF16, "z_a")
        interleave(rows_a, z_a)
        right_late = pick_right(1, late, 256, "rows_a")
        q_a = quantize_z(z_a, "q_a")
        second_product(0, 1, (q_a[0], q_a[1], 0))
        pick_left(1, late, right_late, diff_c, 384)
        store(0, (0,))
        for t in (2, 3):
            bound_rows(diff_c, t, t + 1, f"th_c{t}", [(rows_c, 0, P)])
        store(0, (1, 2))
        z_b = tile([P, P, PACK], BF16, "z_b", "rows_a")
        interleave(rows_b, z_b)
        q_b = quantize_z(z_b, "q_b")
        second_product(1, 1, (q_b[0], q_b[1], 0))
        z_c = tile([P, P, PACK], BF16, "z_c")
        interleave(rows_c, z_c)
        q_c = quantize_z(z_c, "q_c")
        store(1, (0, 1))
        second_product(2, 1, (q_c[0], q_c[1], 0))
        store(2, (0, 1))
